import numpy as np
import ml_dtypes


def mxq(x, axis, fmt="e4m3"):
    dtype, down = {"e4m3": (ml_dtypes.float8_e4m3fn, 7), "e5m2": (ml_dtypes.float8_e5m2, 14)}[fmt]
    v = np.moveaxis(np.asarray(x, np.float32).astype(ml_dtypes.bfloat16).astype(np.float64), axis, -1)
    blocks = v.reshape(v.shape[:-1] + (-1, 32))
    amax = np.abs(blocks).max(-1, keepdims=True)
    byte = np.maximum(np.where(amax > 0, np.frexp(amax)[1] - 1 + 127, 0) - down, 1)
    scale = np.exp2(byte - 127.0)
    codes = (blocks / scale).astype(np.float32).astype(dtype).astype(np.float64)
    return np.moveaxis((codes * scale).reshape(v.shape), -1, axis)


WIDE = False


def mx_kscale(k):
    if not WIDE:
        return np.ones(k)
    levels = np.array([10, -10, 5, -5, 0])
    if k % 512:
        return np.exp2(np.random.permutation(np.resize(levels, k // 32))).repeat(32)
    a = np.empty((k // 512, 16))
    for p in range(k // 512):
        a[p, :8] = np.random.permutation(np.resize(levels, 8))
        for g in range(8):
            far = levels[np.abs(levels - a[p, g]) >= 10]
            a[p, g + 8] = far[np.random.randint(len(far))]
    return np.exp2(a.ravel()).repeat(32)


BF16 = ml_dtypes.bfloat16


def bf(x):
    return np.asarray(x, np.float32).astype(BF16)


def f64(x):
    return np.asarray(x).astype(np.float64)


M, J, KT, KA, KV, R = 1536, 1024, 1024, 512, 1024, 1024

EPS = 0.1


def setup_inputs():
    st, sa, sv = mx_kscale(KT), mx_kscale(KA), mx_kscale(KV)
    t = mx_kscale(R)
    return {"text": bf(np.random.standard_normal((M, KT)) * st),
            "audio": bf(np.random.standard_normal((J, KA)) * sa),
            "video": bf(np.random.standard_normal((J, KV)) * sv),
            "u_text": bf(np.random.standard_normal((KT, R)) / np.sqrt(KT) / st[:, None] * t),
            "u_audio": bf(np.random.standard_normal((KA, R)) / np.sqrt(KA) / sa[:, None]),
            "u_video": bf(np.random.standard_normal((KV, R)) / np.sqrt(KV) / sv[:, None]),
            "b_text": bf(0.4 * np.random.standard_normal(R) * t),
            "b_audio": bf(0.5 * np.random.standard_normal(R)),
            "b_video": bf(0.5 * np.random.standard_normal(R)),
            "rank_weight": bf((1 + 0.1 * np.random.standard_normal(R)) / t),
            "prior": bf(0.5 * np.random.standard_normal(J))}


def reference(text, audio, video, u_text, u_audio, u_video, b_text, b_audio, b_video, rank_weight, prior):
    ft = (mxq(f64(text), 1, "e4m3") @ mxq(f64(u_text), 0, "e4m3")) + f64(b_text)
    fa = (mxq(f64(audio), 1, "e4m3") @ mxq(f64(u_audio), 0, "e4m3")) + f64(b_audio)
    fv = (mxq(f64(video), 1, "e4m3") @ mxq(f64(u_video), 0, "e4m3")) + f64(b_video)
    g = fa * fv
    n = g / np.sqrt(np.mean(g * g, axis=1, keepdims=True) + EPS) * f64(rank_weight)
    z = mxq(ft, 1, "e4m3") @ mxq(n, 1, "e4m3").T
    return z / np.sqrt(R) + f64(prior)

from contextlib import ExitStack

import concourse.mybir as mybir
from concourse.masks import make_identity

M, J, KT, KA, KV, R = 1536, 1024, 1024, 512, 1024, 1024
EPS = 0.1
FLOPS = 2 * M * KT * R + 2 * J * KA * R + 2 * J * KV * R + 2 * M * R * J

F32 = mybir.dt.float32
BF16 = mybir.dt.bfloat16
U32 = mybir.dt.uint32
U8 = mybir.dt.uint8
FP8X4 = mybir.dt.float8_e4m3fn_x4
ACT = mybir.ActivationFunctionType
ALU = mybir.AluOpType

P = 128
W = 512
TR = 3
ACC = 4
ROWBUFS = 6
ORDER = [
    ("L", "text", 0,),
    ("L", "text", 1,),
    ("L", "ut", 0, 0,),
    ("L", "ut", 1, 0,),
    ("LV",),
    ("L", "ut", 0, 1,),
    ("L", "ut", 1, 1,),
    ("L", "audio", 0,),
    ("L", "ua", 0, 0,),
    ("L", "uv", 0, 0,),
    ("L", "uv", 1, 0,),
    ("L", "video", 0,),
    ("L", "video", 1,),
    ("L", "text", 2,),
    ("L", "text", 3,),
    ("L", "ua", 0, 1,),
    ("L", "text", 4,),
    ("L", "text", 5,),
    ("T", "t", 0, 0, "S",),
    ("T", "t", 0, 1, "S",),
    ("L", "uv", 0, 1,),
    ("L", "uv", 1, 1,),
    ("L", "audio", 1,),
    ("L", "video", 2,),
    ("L", "video", 3,),
    ("T", "t", 0, 2, "S",),
    ("T", "t", 0, 3, "V",),
    ("WC", "ut", 0, 0, "V",),
    ("TA", 0, 0, "S",),
    ("Q", "t", 0, 0,),
    ("WC", "ut", 1, 0, "S",),
    ("Q", "t", 0, 1,),
    ("VEC",),
    ("FT", 0, 0, 0,),
    ("FT", 0, 0, 1,),
    ("FT", 0, 0, 2,),
    ("FT", 0, 0, 3,),
    ("WC", "ut", 0, 1, "V",),
    ("WC", "ut", 1, 1, "S",),
    ("TA", 0, 1, "V",),
    ("QA", 0,),
    ("T", "v", 0, 0, "S",),
    ("T", "v", 0, 1, "S",),
    ("WC", "ua", 0, 0, "V",),
    ("WC", "uv", 0, 0, "S",),
    ("T", "v", 0, 2, "V",),
    ("T", "v", 0, 3, "V",),
    ("FT", 0, 1, 0,),
    ("FT", 0, 1, 1,),
    ("FT", 0, 1, 2,),
    ("FT", 0, 1, 3,),
    ("Q", "v", 0, 1,),
    ("WC", "uv", 1, 0, "S",),
    ("Q", "v", 0, 0,),
    ("PRI",),
    ("F", 0, 0, 0, "S",),
    ("F", 0, 0, 1, "S",),
    ("T", "t", 1, 0, "S",),
    ("T", "t", 1, 1, "S",),
    ("T", "t", 1, 2, "S",),
    ("T", "t", 1, 3, "S",),
    ("F", 0, 0, 2, "S",),
    ("WC", "uv", 1, 1, "V",),
    ("F", 0, 0, 3, "S",),
    ("O", 0, 0,),
    ("Q", "t", 1, 0,),
    ("Q", "t", 1, 1,),
    ("WC", "ua", 0, 1, "S",),
    ("WC", "uv", 0, 1, "S",),
    ("FT", 1, 0, 0,),
    ("FT", 1, 0, 1,),
    ("FT", 1, 0, 2,),
    ("FT", 1, 0, 3,),
    ("F", 0, 1, 0, "S",),
    ("F", 0, 1, 1, "S",),
    ("F", 0, 1, 2, "S",),
    ("F", 0, 1, 3, "S",),
    ("FT", 1, 1, 0,),
    ("FT", 1, 1, 1,),
    ("FT", 1, 1, 2,),
    ("TA", 1, 0, "V",),
    ("TA", 1, 1, "V",),
    ("T", "v", 1, 0, "S",),
    ("QA", 1,),
    ("T", "v", 1, 1, "S",),
    ("FT", 1, 1, 3,),
    ("T", "v", 1, 2, "S",),
    ("T", "v", 1, 3, "S",),
    ("Q", "v", 1, 0,),
    ("Q", "v", 1, 1,),
    ("O", 0, 1,),
    ("N", 0,),
    ("F", 1, 0, 0, "S",),
    ("F", 1, 0, 1, "S",),
    ("F", 1, 0, 2, "S",),
    ("F", 1, 0, 3, "S",),
    ("O", 1, 0,),
    ("NH", 0, 0,),
    ("NH", 0, 1,),
    ("F", 1, 1, 0, "S",),
    ("F", 1, 1, 1, "S",),
    ("F", 1, 1, 2, "S",),
    ("F", 1, 1, 3, "S",),
    ("T", "t", 2, 0, "V",),
    ("T", "t", 2, 1, "S",),
    ("T", "t", 2, 2, "S",),
    ("T", "t", 2, 3, "V",),
    ("Q", "t", 2, 0,),
    ("Q", "t", 2, 1,),
    ("O", 1, 1,),
    ("Z", 0, 0, 0, "V",),
    ("Z", 0, 1, 0, "V",),
    ("Z", 0, 2, 0, "V",),
    ("Z", 0, 3, 0, "V",),
    ("FS", 2, 0, 0,),
    ("Z", 1, 3, 0, "V",),
    ("FS", 2, 0, 1,),
    ("FS", 2, 0, 2,),
    ("FS", 2, 0, 3,),
    ("N", 1,),
    ("FG", 2, 0, 0, "S",),
    ("Z", 1, 1, 0, "V",),
    ("Z", 1, 2, 0, "V",),
    ("FG", 2, 0, 1, "V",),
    ("Z", 1, 0, 0, "V",),
    ("NH", 1, 0,),
    ("NH", 1, 1,),
    ("FS", 2, 1, 0,),
    ("FS", 2, 1, 1,),
    ("FS", 2, 1, 2,),
    ("FS", 2, 1, 3,),
    ("FG", 2, 1, 0, "S",),
    ("Z", 0, 3, 1, "V",),
    ("Z", 1, 0, 1, "V",),
    ("FG", 2, 1, 1, "S",),
    ("Z", 0, 1, 1, "V",),
    ("Z", 1, 1, 1, "V",),
    ("FG", 2, 1, 2, "S",),
    ("FG", 2, 1, 3, "V",),
    ("Z", 1, 2, 1, "V",),
    ("FG", 2, 0, 2, "S",),
    ("FG", 2, 0, 3, "S",),
    ("Z", 2, 2, 1, "V",),
    ("Z", 1, 3, 1, "V",),
    ("Z", 2, 0, 0, "V",),
    ("Z", 0, 0, 1, "V",),
    ("Z", 2, 1, 0, "V",),
    ("Z", 0, 2, 1, "V",),
    ("Z", 2, 2, 0, "V",),
    ("Z", 2, 3, 0, "V",),
    ("Z", 2, 0, 1, "V",),
    ("Z", 2, 1, 1, "V",),
    ("Z", 2, 3, 1, "V",),
]


def tile_lowrank_trimodal_fusion_f5_kernel(
    tc, text, audio, video, u_text, u_audio, u_video, b_text, b_audio, b_video, rank_weight, prior, out
):
    nc = tc.nc
    with ExitStack() as ctx:
        const = ctx.enter_context(tc.tile_pool(name="const", bufs=1))
        raws = ctx.enter_context(tc.tile_pool(name="raws", bufs=1))
        work = ctx.enter_context(tc.tile_pool(name="work", bufs=1))
        codes = ctx.enter_context(tc.tile_pool(name="codes", bufs=1))
        psum = ctx.enter_context(tc.psum_pool(name="psum", bufs=1))

        ident = const.tile([P, P], F32, name="ident")
        make_identity(nc, ident[:])
        ones = const.tile([P, P], F32, name="ones")
        nc.vector.memset(ones[:], 1.0)
        ones_b = const.tile([P, P], BF16, name="ones_b")
        nc.vector.memset(ones_b[:], 1.0)
        vec_rows = const.tile([P, P], BF16, name="vec_rows")
        nc.vector.memset(vec_rows[:], 0.0)
        prior_row = const.tile([P, J], BF16, name="prior_row")
        nc.gpsimd.memset(prior_row[:], 0.0)
        vec32 = const.tile([P, P], F32, name="vec32")
        vecs = const.tile([P, 32], F32, name="vecs")
        prior_bc = const.tile([P, J], F32, name="prior_bc")

        def row_tile(name, n, k):
            tile = raws.tile([P, n, k], BF16, name=name, tag="rows", bufs=ROWBUFS)
            return tile

        def weight_tile(name):
            tile = raws.tile([P, 4, R], BF16, name=name, tag="uw", bufs=3)
            return tile

        def load_rows(src, name, row, n, k):
            tile = row_tile(name, n, k)
            nc.sync.dma_start(out=tile[:], in_=src[row : row + n * P, :].rearrange("(a p) k -> p a k", p=P))
            return tile

        def load_weight(src, name, g):
            tile = weight_tile(name)
            nc.sync.dma_start(out=tile[:], in_=src[g * W : (g + 1) * W, :].rearrange("(p j) r -> p j r", j=4))
            return tile

        def load_weight_h(src, name, g, h):
            tile = raws.tile([P, 4, W], BF16, name=name, tag="uwh", bufs=6)
            load_weight_half(src, tile, g, h)
            return tile

        def load_weight_half(src, tile, g, h):
            nc.sync.dma_start(
                out=tile[:],
                in_=src[g * W : (g + 1) * W, h * W : (h + 1) * W].rearrange("(p j) r -> p j r", j=4),
            )

        def load_vectors():
            for v, vec in enumerate((b_text, b_audio, b_video, rank_weight)):
                for h in range(2):
                    nc.sync.dma_start(
                        out=vec_rows[v * 8 + h * 4 : v * 8 + h * 4 + 4, :].rearrange("t (q i) -> t q i", i=8),
                        in_=vec[h * W : (h + 1) * W].rearrange("(q t i) -> t q i", t=4, i=8),
                    )
            nc.sync.dma_start(out=prior_row[0:1, :], in_=prior.unsqueeze(0))
        def vec_setup():
            nc.vector.tensor_copy(out=vec32[:], in_=vec_rows[:])
            vec_ps = psum.tile([P, P], F32, name="vec_ps", tag="tr", bufs=TR)
            nc.tensor.transpose(vec_ps[:], vec32[:], ident[:])
            nc.vector.tensor_copy(out=vecs[:], in_=vec_ps[:, 0:32])

        def vec_col(v, h, t):
            c = v * 8 + h * 4 + t
            return vecs[:, c : c + 1]

        def prior_setup():
            for half in range(2):
                pr_ps = psum.tile([P, W], F32, name="pr_ps", tag="acc", bufs=ACC)
                nc.tensor.matmul(
                    pr_ps[:], lhsT=ones_b[:], rhs=prior_row[:, half * W : (half + 1) * W], start=True, stop=True
                )
                nc.scalar.copy(out=prior_bc[:, half * W : (half + 1) * W], in_=pr_ps[:])

        def copy_on(engine, out_ap, in_ap):
            if engine == "V":
                nc.vector.tensor_copy(out=out_ap, in_=in_ap)
            else:
                nc.scalar.copy(out=out_ap, in_=in_ap)

        def transpose_block(raw, a, xt, i, engine):
            words = raw[:, a, :].bitcast(F32)
            bank = psum.tile([P, 4, P], F32, name="bank", tag="tr", bufs=TR)
            for g in range(2):
                for u in range(2):
                    nc.tensor.transpose(
                        bank[:, 2 * g + u, :], words[:, 256 * g + u : 256 * (g + 1) : 2], ident[:]
                    )
            dst = xt[:].rearrange("p g r t -> p (g r t)").bitcast(F32).rearrange("p (g r u) -> p g r u", g=2, u=2)
            copy_on(engine, dst[:, :, i * P : (i + 1) * P, :], bank[:].rearrange("p (g u) r -> p g r u", g=2))

        def transpose_audio(raw, a, xt, engine):
            bank = psum.tile([P, 4, P], F32, name="bank", tag="tr", bufs=TR)
            for i in range(2):
                words = raw[:, a + i, :].bitcast(F32)
                for u in range(2):
                    nc.tensor.transpose(bank[:, 2 * i + u, :], words[:, u:256:2], ident[:])
            dst = xt[:].rearrange("p r t -> p (r t)").bitcast(F32).rearrange("p (i r u) -> p i r u", i=4, u=2)
            copy_on(engine, dst[:, a : a + 2, :, :], bank[:].rearrange("p (i u) r -> p i r u", i=2))

        def quantize(in_ap, code_ap, scale_ap):
            nc.vector.quantize_mx(out=code_ap.bitcast(FP8X4), scales=scale_ap, in_=in_ap)

        def weight_chunk(raw, h_in_raw, code, scale, h, engine):
            grouped = work.tile([P, 4, 4 * P], BF16, name="grouped", tag="grouped", bufs=3, align_bytes=64)
            src = raw[:].rearrange("p j (q t i) -> p t q i j", t=4, i=8)
            dst = grouped[:].rearrange("p t (q i j) -> p t q i j", i=8, j=4)
            if engine == "V":
                nc.vector.tensor_copy(out=dst, in_=src)
            else:
                for t in range(4):
                    nc.scalar.copy(out=dst[:, t], in_=src[:, t])
            quantize(
                grouped[:].rearrange("p t k -> p (t k)"),
                code[:, h * W : (h + 1) * W],
                scale[:, h * W : (h + 1) * W],
            )

        def code_tiles(width, name, tag=None, bufs=1):
            c = codes.tile([P, width], U32, name=name + "_c", tag=(tag or name) + "_c", bufs=bufs, align_bytes=64)
            s = codes.tile([P, width], U8, name=name + "_s", tag=(tag or name) + "_s", bufs=bufs, align_bytes=64)
            return c, s

        def mx(out_ap, lhs, l0, rhs, r0, n, start, stop):
            nc.tensor.matmul_mx(
                out=out_ap,
                lhsT=lhs[0][:, l0 : l0 + P].bitcast(FP8X4),
                lhsT_scale=lhs[1][:, l0 : l0 + P],
                rhs=rhs[0][:, r0 : r0 + n].bitcast(FP8X4),
                rhs_scale=rhs[1][:, r0 : r0 + n],
                start=start,
                stop=stop,
            )

        ua = code_tiles(R, "ua")
        uv = [code_tiles(R, "uv%d" % g) for g in range(2)]
        ut = [code_tiles(R, "ut%d" % g) for g in range(2)]
        nq = [[code_tiles(W, "n%d%d" % (h, jh)) for jh in range(2)] for h in range(2)]

        XT = {}
        XQ = {}

        def tile_wide(key, raw, a, i, engine):
            if i == 0:
                xt = work.tile([P, 2, W, 4], BF16, name="xt", tag="xt", bufs=2, align_bytes=64)
                XT[key] = xt
            transpose_block(raw, a, XT[key], i, engine)

        def quant_wide(key, g, bufs=2):
            q = code_tiles(W, "xq%d" % g, tag="xq%d" % g, bufs=bufs)
            quantize(XT[key][:, g].rearrange("p r t -> p (r t)"), q[0][:], q[1][:])
            XQ[key, g] = q

        def pair_audio(key, raw, a, engine):
            if a == 0:
                xa = work.tile([P, W, 4], BF16, name="xa", tag="xa", bufs=1, align_bytes=64)
                XT[key] = xa
            transpose_audio(raw, a, XT[key], engine)

        def quant_audio(key):
            q = code_tiles(W, "aq", tag="aq", bufs=2)
            quantize(XT[key][:].rearrange("p r t -> p (r t)"), q[0][:], q[1][:])
            XQ[key] = q

        FTG = {}
        FQ = {}

        def ft_mm(sb, h, mb):
            if mb == 0:
                ftg = work.tile([P, W, 4], BF16, name="ftg", tag="ftg", bufs=2, align_bytes=64)
                FTG[sb, h] = ftg
            bank = psum.tile([P, 4, P], F32, name="ftb", tag="acc", bufs=ACC)
            for t in range(4):
                for g in range(2):
                    mx(bank[:, t, :], ut[g], h * W + t * P, XQ["t%d" % sb, g], mb * P, P, g == 0, g == 1)
            nc.vector.tensor_tensor(
                out=FTG[sb, h][:, mb * P : (mb + 1) * P, :],
                in0=bank[:].rearrange("p t m -> p m t"),
                in1=vecs[:, h * 4 : h * 4 + 4].unsqueeze(1).to_broadcast([P, P, 4]),
                op=ALU.add,
            )
            if mb == 3:
                q = code_tiles(W, "fq%d%d" % (sb, h))
                FQ[sb, h] = q
                quantize(FTG[sb, h][:].rearrange("p m t -> p (m t)"), q[0][:], q[1][:])

        FB = {}

        def ft_wide(sb, h, t):
            if t == 0:
                fb = work.tile([P, 4, W], BF16, name="fb", tag="grouped", bufs=3, align_bytes=64)
                FB[sb, h] = fb
            bank = psum.tile([P, W], F32, name="ftw", tag="acc", bufs=ACC)
            for g in range(2):
                mx(bank[:], ut[g], h * W + t * P, XQ["t%d" % sb, g], 0, W, g == 0, g == 1)
            nc.scalar.activation(out=FB[sb, h][:, t, :], in_=bank[:], func=ACT.Identity, bias=vec_col(0, h, t))

        def ft_inter(sb, h, mb, engine):
            if mb == 0:
                ftg = work.tile([P, W, 4], BF16, name="ftg", tag="ftg", bufs=2, align_bytes=64)
                FTG[sb, h] = ftg
            ms = slice(mb * P, (mb + 1) * P)
            src = FB[sb, h][:, :, ms].rearrange("p t m -> p m t")
            if engine == "G":
                nc.gpsimd.tensor_scalar(
                    out=FTG[sb, h][:, ms, :], in0=src, scalar1=1.0, scalar2=0.0, op0=ALU.mult, op1=ALU.add
                )
            else:
                copy_on(engine, FTG[sb, h][:, ms, :], src)
            if mb == 3:
                q = code_tiles(W, "fq%d%d" % (sb, h))
                FQ[sb, h] = q
                quantize(FTG[sb, h][:].rearrange("p m t -> p (m t)"), q[0][:], q[1][:])

        GW = {}
        SS = {0: [], 1: []}

        SQ = {}
        PAIR = {}
        SSB = {}

        def factor(jh, h, t, wx):
            if t == 0:
                gw = work.tile([P, 4, W], F32, name="gw", tag="gw", bufs=3)
                GW[jh, h] = gw
            gw = GW[jh, h]
            col = h * W + t * P
            fa = psum.tile([P, W], F32, name="fa", tag="acc", bufs=ACC)
            mx(fa[:], ua, col, XQ["a%d" % jh], 0, W, True, True)
            fab = work.tile([P, W], F32, name="fab", tag="fab", bufs=3)
            nc.scalar.activation(out=fab[:], in_=fa[:], func=ACT.Identity, bias=vec_col(1, h, t))
            fv = psum.tile([P, W], F32, name="fv", tag="acc", bufs=ACC)
            for g in range(2):
                mx(fv[:], uv[g], col, XQ["v%d" % jh, g], 0, W, g == 0, g == 1)
            nc.vector.scalar_tensor_tensor(
                out=gw[:, t, :], in0=fv[:], scalar=vec_col(2, h, t), in1=fab[:], op0=ALU.add, op1=ALU.mult
            )
            if t % 2 == 1:
                sq = work.tile([P, 2, W], F32, name="sq", tag="sq", bufs=2)
                nc.scalar.activation(out=sq[:], in_=gw[:, t - 1 : t + 1, :], func=ACT.Square)
                SQ[jh, h, t] = sq
                for tt in (t - 1, t):
                    if wx == "G":
                        nc.gpsimd.tensor_scalar(
                            out=gw[:, tt, :],
                            in0=gw[:, tt, :],
                            scalar1=vec_col(3, h, tt),
                            scalar2=0.0,
                            op0=ALU.mult,
                            op1=ALU.add,
                        )
                    else:
                        nc.scalar.activation(
                            out=gw[:, tt, :], in_=gw[:, tt, :], func=ACT.Copy, scale=vec_col(3, h, tt)
                        )
            if t == 3:
                pair = work.tile([P, 2, W], F32, name="pair", tag="pair", bufs=2)
                nc.vector.tensor_tensor(out=pair[:], in0=SQ[jh, h, 1][:], in1=SQ[jh, h, 3][:], op=ALU.add)
                PAIR[jh, h] = pair

        def ones_sum(jh, h):
            if h == 0:
                ssb = psum.tile([P, W], F32, name="ssb", tag="ss", bufs=1)
                SSB[jh] = ssb
            for i in range(2):
                nc.tensor.matmul(
                    SSB[jh][:],
                    lhsT=ones[:],
                    rhs=PAIR[jh, h][:, i, :],
                    start=(h == 0 and i == 0),
                    stop=(h == 1 and i == 1),
                )

        RSTD = {}

        def norm(jh):
            rstd = work.tile([P, W], F32, name="rstd", tag="rstd", bufs=1)
            nc.scalar.activation(
                out=rstd[:], in_=SSB[jh][:], func=ACT.Abs_reciprocal_sqrt, scale=1.0 / R, bias=EPS
            )
            RSTD[jh] = rstd

        def n_half(jh, h):
            nt = work.tile([P, W, 4], BF16, name="nt", tag="nt", bufs=2, align_bytes=64)
            nc.vector.tensor_tensor(
                out=nt[:],
                in0=GW[jh, h][:].rearrange("p t j -> p j t"),
                in1=RSTD[jh][:].unsqueeze(2).to_broadcast([P, W, 4]),
                op=ALU.mult,
            )
            quantize(nt[:].rearrange("p j t -> p (j t)"), nq[h][jh][0][:], nq[h][jh][1][:])

        def z_one(sb, ib, jh, engine):
            z = psum.tile([P, W], F32, name="z", tag="acc", bufs=ACC)
            for h in range(2):
                mx(z[:], FQ[sb, h], ib * P, nq[h][jh], 0, W, h == 0, h == 1)
            cols = slice(jh * W, (jh + 1) * W)
            ot = work.tile([P, W], F32, name="ot", tag="ot", bufs=6)
            if engine == "S":
                zs = work.tile([P, W], F32, name="zs", tag="zs", bufs=2)
                nc.scalar.activation(out=zs[:], in_=z[:], func=ACT.Copy, scale=1.0 / 32.0)
                nc.gpsimd.tensor_tensor(out=ot[:], in0=zs[:], in1=prior_bc[:, cols], op=ALU.add)
            else:
                nc.vector.scalar_tensor_tensor(
                    out=ot[:], in0=z[:], scalar=1.0 / 32.0, in1=prior_bc[:, cols], op0=ALU.mult, op1=ALU.add
                )
            row = sb * W + ib * P
            nc.sync.dma_start(out=out[row : row + P, cols], in_=ot[:])


        text_raw = {}
        video_raw = {}
        audio_raw = {}
        UT = {}
        def run(tok):
            k = tok[0]
            if k == "LV":
                load_vectors(); UT["LV"] = True
            elif k == "L":
                w, i = tok[1], tok[2]
                if w == "text": text_raw[i] = load_rows(text, "text_raw%d" % i, i * 256, 2, KT)
                elif w == "video": video_raw[i] = load_rows(video, "video_raw%d" % i, i * 256, 2, KV)
                elif w == "audio": audio_raw[i] = load_rows(audio, "audio_raw%d" % i, i * 512, 4, KA)
                else: UT["raw", w, i, tok[3]] = load_weight_h({"ut": u_text, "uv": u_video, "ua": u_audio}[w], "%s_raw%d%d" % (w, i, tok[3]), i, tok[3])
            elif k == "T":
                w, blk, i, e = tok[1:]
                raw = (text_raw if w == "t" else video_raw)[blk * 2 + i // 2]
                assert i == 0 or UT["T", w, blk, i - 1]
                UT["T", w, blk, i] = True
                tile_wide("%s%d" % (w, blk), raw, i % 2, i, e)
            elif k == "Q":
                UT["T", tok[1], tok[2], 3]
                quant_wide("%s%d" % (tok[1], tok[2]), tok[3])
            elif k == "TA":
                assert tok[2] == 0 or UT["TA", tok[1], 0]
                UT["TA", tok[1], tok[2]] = True
                pair_audio("a%d" % tok[1], audio_raw[tok[1]], tok[2] * 2, tok[3])
            elif k == "QA":
                UT["TA", tok[1], 1]
                quant_audio("a%d" % tok[1])
            elif k == "WC":
                w, g, h, e = tok[1:]
                c = {"ut": ut, "uv": uv, "ua": [ua]}[w][g]
                weight_chunk(UT["raw", w, g, h], h, c[0], c[1], h, e)
                UT[w, g, h] = True
            elif k == "VEC": UT["LV"]; vec_setup(); UT["vec"] = True
            elif k == "PRI": UT["LV"]; prior_setup(); UT["pri"] = True
            elif k == "FT":
                sb, h, mb = tok[1:]
                UT["vec"]; UT["ut", 0, h]; UT["ut", 1, h]
                assert mb == 0 or UT["ft", sb, h, mb - 1]
                UT["ft", sb, h, mb] = True
                ft_mm(sb, h, mb)
            elif k == "FS":
                sb, h, t = tok[1:]
                UT["vec"]; UT["ut", 0, h]; UT["ut", 1, h]
                assert t == 0 or UT["fs", sb, h, t - 1]
                UT["fs", sb, h, t] = True
                ft_wide(sb, h, t)
            elif k == "FG":
                sb, h, mb = tok[1:4]
                UT["fs", sb, h, 3]
                assert mb == 0 or UT["ft", sb, h, mb - 1]
                UT["ft", sb, h, mb] = True
                ft_inter(sb, h, mb, tok[4])
            elif k == "F":
                jh, h, t = tok[1:4]
                assert (h == 0 and t == 0) or UT["f", jh, h if t else 0, (t - 1) % 4]
                UT["vec"]; UT["uv", 0, h]; UT["uv", 1, h]; UT["ua", 0, h]
                factor(jh, h, t, tok[4])
                UT["f", jh, h, t] = True
            elif k == "O":
                UT["f", tok[1], tok[2], 3]
                assert tok[2] == 0 or UT["o", tok[1], 0]
                assert tok[1] == 0 or tok[2] == 1 or UT["N", 0]
                UT["o", tok[1], tok[2]] = True
                ones_sum(tok[1], tok[2])
            elif k == "N":
                UT["o", tok[1], 1]
                UT["N", tok[1]] = True
                assert tok[1] == 0 or UT["n", 0, 0] and UT["n", 0, 1]
                norm(tok[1])
            elif k == "NH":
                n_half(tok[1], tok[2]); UT["n", tok[1], tok[2]] = True
            elif k == "Z":
                sb, ib, jh, e = tok[1:]
                UT["n", jh, 0]; UT["n", jh, 1]; UT["pri"]
                z_one(sb, ib, jh, e)
            else: raise ValueError(k)
        for tok in ORDER: run(tok)
